import numpy as np
import ml_dtypes


def mxq(x, axis, fmt="e4m3"):
    dtype, down = {"e4m3": (ml_dtypes.float8_e4m3fn, 7), "e5m2": (ml_dtypes.float8_e5m2, 14)}[fmt]
    v = np.moveaxis(np.asarray(x, np.float32).astype(ml_dtypes.bfloat16).astype(np.float64), axis, -1)
    blocks = v.reshape(v.shape[:-1] + (-1, 32))
    amax = np.abs(blocks).max(-1, keepdims=True)
    byte = np.maximum(np.where(amax > 0, np.frexp(amax)[1] - 1 + 127, 0) - down, 1)
    scale = np.exp2(byte - 127.0)
    codes = (blocks / scale).astype(np.float32).astype(dtype).astype(np.float64)
    return np.moveaxis((codes * scale).reshape(v.shape), -1, axis)


WIDE = False


def mx_kscale(k):
    if not WIDE:
        return np.ones(k)
    levels = np.array([10, -10, 5, -5, 0])
    if k % 512:
        return np.exp2(np.random.permutation(np.resize(levels, k // 32))).repeat(32)
    a = np.empty((k // 512, 16))
    for p in range(k // 512):
        a[p, :8] = np.random.permutation(np.resize(levels, 8))
        for g in range(8):
            far = levels[np.abs(levels - a[p, g]) >= 10]
            a[p, g + 8] = far[np.random.randint(len(far))]
    return np.exp2(a.ravel()).repeat(32)


def f64(x):
    return np.asarray(x).astype(np.float64)


def striped(idx):
    return np.tile(idx.reshape(-1, 16).T, (8, 1)).astype(np.uint16)


def unstriped(offs):
    return offs[:16].T.reshape(-1).astype(np.int64)


def pack_weight(w):
    k, n = w.shape
    w = f64(np.asarray(w, np.float32).astype(ml_dtypes.bfloat16)).reshape(k // 32, 32, n)
    amax = np.abs(w).max(1)
    byte = np.clip(np.where(amax > 0, np.frexp(amax)[1] - 1 + 127 - 7, 1), 1, 254)
    scaled = (w * np.exp2(127.0 - byte)[:, None, :]).reshape(k, n).astype(np.float32)
    words = np.ascontiguousarray(scaled.reshape(k // 512, 128, 4, n).transpose(0, 1, 3, 2)).astype(ml_dtypes.float8_e4m3fn).view(np.uint8)
    return words, np.ascontiguousarray(byte.astype(np.uint8).reshape(k // 512, 16, n))


def unpack_weight(words, scales):
    g, p, n, _ = words.shape
    vals = np.ascontiguousarray(words).view(ml_dtypes.float8_e4m3fn).astype(np.float64) * np.repeat(np.exp2(scales.astype(np.float64) - 127.0), 8, axis=1)[..., None]
    return vals.transpose(0, 1, 3, 2).reshape(g * 512, n)


def gelu(v):
    return 0.5 * v * (1.0 + np.tanh(np.sqrt(2.0 / np.pi) * (v + 0.044715 * v**3)))


K, T, S, H, N, U = 512, 2048, 512, 512, 256, 1024


def setup_inputs():
    n = np.random.standard_normal
    s = mx_kscale(K)[:, None]
    u = mx_kscale(H)
    packed_w2 = pack_weight(n((H, N)) / np.sqrt(H) / u[:, None])
    return {
        "xT": (n((K, T)) * s).astype(np.float32),
        "w1": (n((K, H)) / np.sqrt(K) / s * u).astype(np.float32),
        "w2_words": packed_w2[0],
        "w2_scales": packed_w2[1],
        "skip": (n((H, U)) * u[:, None]).astype(np.float32),
        "offs": striped(np.random.permutation(T)[:S]),
        "cell": striped(np.random.permutation(U)[:S]),
    }


def reference(xT, w1, w2_words, w2_scales, skip, offs, cell):
    xq = mxq(f64(xT)[:, unstriped(offs)], 0, "e4m3")
    up = np.zeros((H, U))
    up[:, unstriped(cell)] = gelu(mxq(f64(w1), 0, "e4m3").T @ xq)
    z = up + f64(skip)
    return unpack_weight(w2_words, w2_scales).T @ mxq(z, 0, "e4m3")

@@ -1,0 +1,237 @@
+from contextlib import ExitStack
+
+import concourse.mybir as mybir
+from concourse.masks import make_identity
+
+K, T, S, H, N, U = 512, 2048, 512, 512, 256, 1024
+FLOPS = 2 * K * H * S + 2 * H * N * U
+
+F32 = mybir.dt.float32
+BF16 = mybir.dt.bfloat16
+I32 = mybir.dt.int32
+U32 = mybir.dt.uint32
+U16 = mybir.dt.uint16
+U8 = mybir.dt.uint8
+FP8X4 = mybir.dt.float8_e4m3fn_x4
+GELU = mybir.ActivationFunctionType.Gelu_apprx_tanh
+ADD = mybir.AluOpType.add
+
+P = 128
+PACK = 4
+HALF = S // 2
+HC = HALF // 16
+CH = 256
+NCH = U // CH
+BANK = 512
+
+
+def tile_picked_unet_gelu_e_kernel(tc, xT, w1, w2_words, w2_scales, skip, offs, cell, out):
+    nc = tc.nc
+    with ExitStack() as ctx:
+        sb = ctx.enter_context(tc.tile_pool(name="sb", bufs=1))
+        ps = ctx.enter_context(tc.psum_pool(name="ps", bufs=1))
+
+        def bank(b, name, shape=(P, BANK)):
+            return ps.tile(list(shape), F32, name=name, tag="bank%d" % b)
+
+        offs_sb = sb.tile([P, S // 16], U16, name="offs_sb")
+        cell_sb = sb.tile([P, S // 16], U16, name="cell_sb")
+        x_sb = [sb.tile([P, T], F32, name="x%d" % j) for j in range(PACK)]
+        w1_sb = [sb.tile([P, PACK, H // 2], F32, name="w1_%d" % h) for h in range(2)]
+        names = ["A", "C", "B", "D"]
+        skip_sb = dict((n, sb.tile([P, U], F32, name="skip" + n)) for n in names)
+        up = dict((n, sb.tile([P, U], F32, name="up" + n)) for n in names)
+        w2c = sb.tile([P, N], U32, name="w2c", align_bytes=64)
+        w2s = sb.tile([P, N], U8, name="w2s", align_bytes=64)
+        ztc = [sb.tile([P, 4, P], F32, name="ztc%d" % b) for b in range(2)]
+        warm = sb.tile([P, 8], F32, name="warm")
+        warm2 = sb.tile([P, 8], F32, name="warm2")
+        ident = sb.tile([P, P], F32, name="ident")
+
+        x_rows = xT.rearrange("(p j) t -> p j t", j=PACK)
+        w1_rows = w1.rearrange("(p j) c -> p j c", j=PACK)
+        skip_rows = skip.rearrange("(p t) u -> p t u", t=PACK)
+
+        nc.vector.memset(warm[:], 0.0)
+        nc.scalar.activation(warm2[:], warm[:], GELU)
+        nc.vector.memset(w2s[:].bitcast(I32), 0)
+        for n in names:
+            nc.vector.memset(up[n][:], 0.0)
+        for b in range(2):
+            nc.vector.memset(ztc[b][:], 0.0)
+        make_identity(nc, ident[:])
+
+        nc.sync.dma_start(x_sb[0][:], x_rows[:, 0, :])
+        nc.sync.dma_start(offs_sb[:], offs)
+        nc.sync.dma_start(w1_sb[0][:], w1_rows[:, :, 0 : H // 2])
+        nc.sync.dma_start(x_sb[1][:], x_rows[:, 1, :])
+        nc.sync.dma_start(x_sb[2][:], x_rows[:, 2, :])
+        nc.sync.dma_start(cell_sb[:], cell)
+        nc.sync.dma_start(x_sb[3][:], x_rows[:, 3, :])
+        nc.sync.dma_start(w1_sb[1][:], w1_rows[:, :, H // 2 : H])
+        for n, h in (("A", 0), ("C", None), ("B", 1), ("D", None)):
+            if h is None:
+                nc.sync.dma_start(skip_sb[n][:], skip_rows[:, 3 if n == "C" else 2, :])
+            else:
+                for e in range(2):
+                    nc.sync.dma_start(skip_sb[n][64 * e : 64 * e + 64, :], skip_rows[64 * h : 64 * h + 64, e, :])
+        nc.sync.dma_start(w2c[:].bitcast(I32), w2_words[0].rearrange("p n t -> p (n t)").bitcast(I32))
+        for q in range(4):
+            nc.sync.dma_start(w2s[32 * q : 32 * q + 4, :].bitcast(I32), w2_scales[0, 4 * q : 4 * q + 4, :].bitcast(I32))
+
+        wg_pair = [sb.tile([P, P, PACK], BF16, name="wgp%d" % h, align_bytes=64) for h in range(2)]
+        wg_cd = sb.tile([P, 2 * P, PACK], BF16, name="wgcd", align_bytes=64)
+        wc_pair = [sb.tile([P, P], U32, name="wcp%d" % h, align_bytes=64) for h in range(2)]
+        ws_pair = [sb.tile([P, P], U8, name="wsp%d" % h, align_bytes=64) for h in range(2)]
+        wc_cd = sb.tile([P, 2 * P], U32, name="wccd", align_bytes=64)
+        ws_cd = sb.tile([P, 2 * P], U8, name="wscd", align_bytes=64)
+
+        def w_src(h):
+            return w1_sb[h][:].rearrange("p j (m t) -> p m j t", t=PACK)
+
+        def w_copy_pair(h):
+            nc.scalar.copy(wg_pair[h][:].rearrange("p (e m) j -> p m j e", e=2), w_src(h)[:, :, :, 0:2])
+
+        def w_copy_cd(h):
+            dst = wg_cd[:].rearrange("p (s h m) j -> p h m j s", s=2, h=2)
+            nc.scalar.copy(dst[:, h], w_src(h)[:, :, :, 2:4])
+
+        def quant(codes, scales, src):
+            nc.vector.quantize_mx(out=codes.bitcast(FP8X4), scales=scales, in_=src)
+
+        w_copy_pair(0)
+        w_copy_cd(0)
+        quant(wc_pair[0][:], ws_pair[0][:], wg_pair[0][:].rearrange("p c j -> p (c j)"))
+
+        xg = [sb.tile([P, HALF, PACK], BF16, name="xg%d" % a, align_bytes=64) for a in range(2)]
+        xc = sb.tile([P, S], U32, name="xc", align_bytes=64)
+        xs = sb.tile([P, S], U8, name="xs", align_bytes=64)
+        for j in range(PACK):
+            for a in range(2):
+                nc.vector.tensor_copy(xg[a][:, :, j], x_sb[j][:].indirect(offs_sb[:, a * HC : (a + 1) * HC]))
+                if j == PACK - 1:
+                    cols = slice(a * HALF, (a + 1) * HALF)
+                    quant(xc[:, cols], xs[:, cols], xg[a][:].rearrange("p c j -> p (c j)"))
+
+        def layer1(acc, wc, ws, cols):
+            nc.tensor.matmul_mx(out=acc, lhsT=wc.bitcast(FP8X4), lhsT_scale=ws, rhs=xc[:, cols].bitcast(FP8X4), rhs_scale=xs[:, cols], start=True, stop=True)
+
+        h_a = [sb.tile([P, HALF], F32, name="hA%d" % a) for a in range(2)]
+        for a in range(2):
+            acc = bank(a, "accA%d" % a, (P, HALF))
+            layer1(acc[:], wc_pair[0][:], ws_pair[0][:], slice(a * HALF, (a + 1) * HALF))
+            nc.scalar.activation(h_a[a][:], acc[:], GELU)
+        for a in range(2):
+            nc.vector.tensor_copy(up["A"][:].indirect(cell_sb[:, a * HC : (a + 1) * HC]), h_a[a][:])
+
+        w_copy_cd(1)
+        quant(wc_cd[:], ws_cd[:], wg_cd[:].rearrange("p c j -> p (c j)"))
+        w_copy_pair(1)
+        quant(wc_pair[1][:], ws_pair[1][:], wg_pair[1][:].rearrange("p c j -> p (c j)"))
+
+        hs = {}
+        for n, b, wc, ws in (("C", 2, wc_cd[:, P : 2 * P], ws_cd[:, P : 2 * P]), ("B", 3, wc_pair[1][:], ws_pair[1][:]), ("D", 3, wc_cd[:, 0:P], ws_cd[:, 0:P])):
+            acc = bank(b, "acc" + n)
+            layer1(acc[:], wc, ws, slice(0, S))
+            hs[n] = sb.tile([P, S], F32, name="h" + n)
+            nc.scalar.activation(hs[n][:], acc[:], GELU)
+
+        def turn_sum(n, banks):
+            sums = []
+            for half, b in enumerate(banks):
+                acc = bank(b, "sum%s%d" % (n, half), (P, 4, P))
+                for i in range(4):
+                    cells = slice(half * BANK + i * P, half * BANK + (i + 1) * P)
+                    nc.tensor.matmul(acc[:, i, :], skip_sb[n][:, cells], ident[:], start=(i == 0), stop=False, is_transpose=True)
+                sums.append(acc)
+            for half, acc in enumerate(sums):
+                for i in range(4):
+                    cells = slice(half * BANK + i * P, half * BANK + (i + 1) * P)
+                    nc.tensor.matmul(acc[:, i, :], up[n][:, cells], ident[:], start=False, stop=(i == 3), is_transpose=True)
+            return sums
+
+        zt = [sb.tile([P, 4, P], F32, name="zt%d" % b, tag="zt%d" % b, align_bytes=64) for b in range(2)]
+        stage = [sb.tile([P, 2, CH], F32, name="stage%d" % q) for q in range(NCH)]
+
+        def round_pair(h, sums):
+            for b in range(2):
+                dst = zt[b][:].bitcast(BF16).rearrange("c i (h m e) -> c h i m e", h=2, e=2)
+                nc.scalar.copy(dst[:, h], sums[b][:].rearrange("c i (e m) -> c i m e", e=2))
+
+        def turn_back(src, banks, u):
+            for half, b in enumerate(banks):
+                acc = bank(b, "back%d%d" % (u, half))
+                for i in range(4):
+                    nc.tensor.transpose(acc[:, i * P : (i + 1) * P], src[half][:, i, :], ident[:])
+                for r in range(2):
+                    nc.scalar.copy(stage[2 * half + r][:, u, :], acc[:, r * CH : (r + 1) * CH])
+
+        sums_a = turn_sum("A", (2, 3))
+        round_pair(0, sums_a)
+
+        nc.vector.tensor_copy(up["C"][:].indirect(cell_sb[:]), hs["C"][:])
+        sums_c = turn_sum("C", (5, 6))
+        for b in range(2):
+            dst = ztc[b][:].bitcast(BF16).rearrange("c i (m e) -> c i m e", e=2)
+            nc.scalar.copy(dst[:, :, :, 1], sums_c[b][:])
+        turn_back(ztc, (0, 1), 1)
+
+        nc.vector.tensor_copy(up["B"][:].indirect(cell_sb[:]), hs["B"][:])
+        sums_b = turn_sum("B", (5, 6))
+        round_pair(1, sums_b)
+        turn_back(zt, (2, 3), 0)
+
+        nc.vector.tensor_copy(up["D"][:].indirect(cell_sb[:]), hs["D"][:])
+
+        zg_all = sb.tile([P, 2 * U], F32, name="zg_all", tag="zt1", align_bytes=64)
+        zg = [zg_all[:, 2 * CH * q : 2 * CH * (q + 1)] for q in range(NCH)]
+        zc = [sb.tile([P, CH], U32, name="zc%d" % q, align_bytes=64) for q in range(NCH)]
+        zs = [sb.tile([P, CH], U8, name="zs%d" % q, align_bytes=64) for q in range(NCH)]
+        out_rows = out.rearrange("(a m) v -> m a v", a=2)
+
+        def add_last(q):
+            cells = slice(q * CH, (q + 1) * CH)
+            dst = stage[q][:, 1, :].bitcast(BF16).rearrange("p (c e) -> p c e", e=2)
+            nc.vector.tensor_tensor(dst[:, :, 0], up["D"][:, cells], skip_sb["D"][:, cells], ADD)
+
+        def weave(q):
+            nc.scalar.copy(zg[q].rearrange("p (c u) -> p c u", u=2), stage[q][:].rearrange("p u c -> p c u"))
+
+        def quant_z(q):
+            quant(zc[q][:], zs[q][:], zg[q].bitcast(BF16))
+
+        def mm2(acc, a, q):
+            m = slice(a * P, (a + 1) * P)
+            nc.tensor.matmul_mx(out=acc, lhsT=w2c[:, m].bitcast(FP8X4), lhsT_scale=w2s[:, m], rhs=zc[q][:].bitcast(FP8X4), rhs_scale=zs[q][:], start=True, stop=True)
+
+        def layer2(q, b, on_vector):
+            acc = bank(b, "o%d" % q, (P, 2, CH))
+            for a in range(2):
+                mm2(acc[:, a, :], a, q)
+            res = sb.tile([P, 2, CH], F32, name="res%d" % q)
+            if on_vector:
+                nc.vector.tensor_copy(res[:], acc[:])
+            else:
+                nc.scalar.copy(res[:], acc[:])
+            nc.sync.dma_start(out_rows[:, :, q * CH : (q + 1) * CH], res[:])
+
+        def layer2_split(q, banks):
+            for a in range(2):
+                acc = bank(banks[a], "o%d%d" % (q, a), (P, CH))
+                mm2(acc[:], a, q)
+                res = sb.tile([P, CH], F32, name="res%d%d" % (q, a))
+                if a == 0:
+                    nc.scalar.copy(res[:], acc[:])
+                else:
+                    nc.vector.tensor_copy(res[:], acc[:])
+                nc.sync.dma_start(out_rows[:, a, q * CH : (q + 1) * CH], res[:])
+
+        for q in range(NCH):
+            add_last(q)
+            weave(q)
+        for q in range(NCH):
+            quant_z(q)
+        layer2(0, 7, False)
+        layer2(1, 4, True)
+        layer2(2, 0, False)
+        layer2_split(3, (1, 5))

@@ -18,11 +18,16 @@ ADD = mybir.AluOpType.add
 
 P = 128
 PACK = 4
-HALF = S // 2
-HC = HALF // 16
-CH = 256
-NCH = U // CH
+GROUP = 16
+HALF_P = P // 2
+PIECE = S // 2
 BANK = 512
+TURNS = BANK // P
+CHUNK = 256
+CHUNKS = U // CHUNK
+LINE = 4
+MX_ALIGN = 64
+ROW_TILES = ("lo", "plane3", "hi", "plane2")
 
 
 def tile_picked_unet_gelu_e_kernel(tc, xT, w1, w2_words, w2_scales, skip, offs, cell, out):
@@ -34,204 +39,198 @@ def tile_picked_unet_gelu_e_kernel(tc, xT, w1, w2_words, w2_scales, skip, offs, 
         def bank(b, name, shape=(P, BANK)):
             return ps.tile(list(shape), F32, name=name, tag="bank%d" % b)
 
-        offs_sb = sb.tile([P, S // 16], U16, name="offs_sb")
-        cell_sb = sb.tile([P, S // 16], U16, name="cell_sb")
+        def quantise(codes, scales, values):
+            nc.vector.quantize_mx(out=codes.bitcast(FP8X4), scales=scales, in_=values)
+
+        def list_piece(lists, a):
+            return lists[:, a * PIECE // GROUP : (a + 1) * PIECE // GROUP]
+
+        offs_sb = sb.tile([P, S // GROUP], U16, name="offs_sb")
+        cell_sb = sb.tile([P, S // GROUP], U16, name="cell_sb")
         x_sb = [sb.tile([P, T], F32, name="x%d" % j) for j in range(PACK)]
-        w1_sb = [sb.tile([P, PACK, H // 2], F32, name="w1_%d" % h) for h in range(2)]
-        names = ["A", "C", "B", "D"]
-        skip_sb = dict((n, sb.tile([P, U], F32, name="skip" + n)) for n in names)
-        up = dict((n, sb.tile([P, U], F32, name="up" + n)) for n in names)
-        w2c = sb.tile([P, N], U32, name="w2c", align_bytes=64)
-        w2s = sb.tile([P, N], U8, name="w2s", align_bytes=64)
-        ztc = [sb.tile([P, 4, P], F32, name="ztc%d" % b) for b in range(2)]
-        warm = sb.tile([P, 8], F32, name="warm")
-        warm2 = sb.tile([P, 8], F32, name="warm2")
+        w1_sb = [sb.tile([P, PACK, H // 2], F32, name="w1_%d" % h, tag="w1_%d" % h, align_bytes=MX_ALIGN) for h in range(2)]
+        skip_pair = dict((n, sb.tile([P, U], F32, name="skip_" + n)) for n in ("lo", "hi"))
+        skip_23 = sb.tile([P, 2, U], F32, name="skip_23")
+        up = dict((n, sb.tile([P, 2 * U if n == "plane2" else U], F32, name="up_" + n)) for n in ROW_TILES)
+        w2_codes = sb.tile([P, N], U32, name="w2_codes", align_bytes=MX_ALIGN)
+        w2_scale = sb.tile([P, N], U8, name="w2_scale", align_bytes=MX_ALIGN)
+        zero = sb.tile([P, 1], F32, name="zero")
+        no_bias = sb.tile([P, 1], F32, name="no_bias")
         ident = sb.tile([P, P], F32, name="ident")
 
         x_rows = xT.rearrange("(p j) t -> p j t", j=PACK)
         w1_rows = w1.rearrange("(p j) c -> p j c", j=PACK)
         skip_rows = skip.rearrange("(p t) u -> p t u", t=PACK)
+        out_rows = out.rearrange("(a m) v -> m a v", a=N // P)
 
-        nc.vector.memset(warm[:], 0.0)
-        nc.scalar.activation(warm2[:], warm[:], GELU)
-        nc.vector.memset(w2s[:].bitcast(I32), 0)
-        for n in names:
-            nc.vector.memset(up[n][:], 0.0)
-        for b in range(2):
-            nc.vector.memset(ztc[b][:], 0.0)
+        nc.vector.memset(zero[:], 0.0)
+        nc.scalar.activation(no_bias[:], zero[:], GELU)
+        nc.vector.memset(w2_scale[:].bitcast(I32), 0)
+        for n in ROW_TILES:
+            nc.vector.memset(up[n][:, 0:U], 0.0)
         make_identity(nc, ident[:])
 
         nc.sync.dma_start(x_sb[0][:], x_rows[:, 0, :])
         nc.sync.dma_start(offs_sb[:], offs)
+        for j in range(1, PACK):
+            nc.sync.dma_start(x_sb[j][:], x_rows[:, j, :])
         nc.sync.dma_start(w1_sb[0][:], w1_rows[:, :, 0 : H // 2])
-        nc.sync.dma_start(x_sb[1][:], x_rows[:, 1, :])
-        nc.sync.dma_start(x_sb[2][:], x_rows[:, 2, :])
         nc.sync.dma_start(cell_sb[:], cell)
-        nc.sync.dma_start(x_sb[3][:], x_rows[:, 3, :])
         nc.sync.dma_start(w1_sb[1][:], w1_rows[:, :, H // 2 : H])
-        for n, h in (("A", 0), ("C", None), ("B", 1), ("D", None)):
-            if h is None:
-                nc.sync.dma_start(skip_sb[n][:], skip_rows[:, 3 if n == "C" else 2, :])
-            else:
-                for e in range(2):
-                    nc.sync.dma_start(skip_sb[n][64 * e : 64 * e + 64, :], skip_rows[64 * h : 64 * h + 64, e, :])
-        nc.sync.dma_start(w2c[:].bitcast(I32), w2_words[0].rearrange("p n t -> p (n t)").bitcast(I32))
+        for h, n in enumerate(("lo", "hi")):
+            for e in range(2):
+                nc.sync.dma_start(skip_pair[n][HALF_P * e : HALF_P * (e + 1), :], skip_rows[HALF_P * h : HALF_P * (h + 1), e, :])
+        nc.sync.dma_start(skip_23[:], skip_rows[:, 2:4, :])
+        nc.sync.dma_start(w2_codes[:].bitcast(I32), w2_words[0].rearrange("p n t -> p (n t)").bitcast(I32))
         for q in range(4):
-            nc.sync.dma_start(w2s[32 * q : 32 * q + 4, :].bitcast(I32), w2_scales[0, 4 * q : 4 * q + 4, :].bitcast(I32))
+            nc.sync.dma_start(w2_scale[32 * q : 32 * q + 4, :].bitcast(I32), w2_scales[0, 4 * q : 4 * q + 4, :].bitcast(I32))
 
-        wg_pair = [sb.tile([P, P, PACK], BF16, name="wgp%d" % h, align_bytes=64) for h in range(2)]
-        wg_cd = sb.tile([P, 2 * P, PACK], BF16, name="wgcd", align_bytes=64)
-        wc_pair = [sb.tile([P, P], U32, name="wcp%d" % h, align_bytes=64) for h in range(2)]
-        ws_pair = [sb.tile([P, P], U8, name="wsp%d" % h, align_bytes=64) for h in range(2)]
-        wc_cd = sb.tile([P, 2 * P], U32, name="wccd", align_bytes=64)
-        ws_cd = sb.tile([P, 2 * P], U8, name="wscd", align_bytes=64)
+        w_bf = [sb.tile([P, PACK, HALF_P, PACK], BF16, name="w_bf%d" % h, align_bytes=MX_ALIGN) for h in range(2)]
+        w1_codes = dict((n, sb.tile([P, P], U32, name="w1_codes_" + n, align_bytes=MX_ALIGN)) for n in ROW_TILES)
+        w1_scale = dict((n, sb.tile([P, P], U8, name="w1_scale_" + n, align_bytes=MX_ALIGN)) for n in ROW_TILES)
 
-        def w_src(h):
-            return w1_sb[h][:].rearrange("p j (m t) -> p m j t", t=PACK)
+        def deal_views(h):
+            return w_bf[h][:].rearrange("p t m j -> p m j t"), w1_sb[h][:].rearrange("p j (m t) -> p m j t", t=PACK)
 
-        def w_copy_pair(h):
-            nc.scalar.copy(wg_pair[h][:].rearrange("p (e m) j -> p m j e", e=2), w_src(h)[:, :, :, 0:2])
+        def quantise_w_pair(h):
+            n = ("lo", "hi")[h]
+            quantise(w1_codes[n][:], w1_scale[n][:], w_bf[h][:, 0:2].rearrange("p t m j -> p (t m j)"))
 
-        def w_copy_cd(h):
-            dst = wg_cd[:].rearrange("p (s h m) j -> p h m j s", s=2, h=2)
-            nc.scalar.copy(dst[:, h], w_src(h)[:, :, :, 2:4])
+        def quantise_w_plane(h, t):
+            n = "plane%d" % t
+            cols = slice(HALF_P * h, HALF_P * (h + 1))
+            quantise(w1_codes[n][:, cols], w1_scale[n][:, cols], w_bf[h][:, t].rearrange("p m j -> p (m j)"))
 
-        def quant(codes, scales, src):
-            nc.vector.quantize_mx(out=codes.bitcast(FP8X4), scales=scales, in_=src)
-
-        w_copy_pair(0)
-        w_copy_cd(0)
-        quant(wc_pair[0][:], ws_pair[0][:], wg_pair[0][:].rearrange("p c j -> p (c j)"))
-
-        xg = [sb.tile([P, HALF, PACK], BF16, name="xg%d" % a, align_bytes=64) for a in range(2)]
-        xc = sb.tile([P, S], U32, name="xc", align_bytes=64)
-        xs = sb.tile([P, S], U8, name="xs", align_bytes=64)
+        x_bf = [sb.tile([P, PIECE, PACK], BF16, name="x_bf%d" % a, align_bytes=MX_ALIGN) for a in range(2)]
+        x_scale = sb.tile([P, S], U8, name="x_scale", align_bytes=MX_ALIGN)
         for j in range(PACK):
             for a in range(2):
-                nc.vector.tensor_copy(xg[a][:, :, j], x_sb[j][:].indirect(offs_sb[:, a * HC : (a + 1) * HC]))
-                if j == PACK - 1:
-                    cols = slice(a * HALF, (a + 1) * HALF)
-                    quant(xc[:, cols], xs[:, cols], xg[a][:].rearrange("p c j -> p (c j)"))
+                picked = sb.tile([P, PIECE], BF16, name="picked%d%d" % (j, a))
+                nc.vector.tensor_copy(picked[:], x_sb[j][:].indirect(list_piece(offs_sb, a)))
+                nc.scalar.copy(x_bf[a][:, :, j], picked[:])
 
-        def layer1(acc, wc, ws, cols):
-            nc.tensor.matmul_mx(out=acc, lhsT=wc.bitcast(FP8X4), lhsT_scale=ws, rhs=xc[:, cols].bitcast(FP8X4), rhs_scale=xs[:, cols], start=True, stop=True)
+        nc.vector.tensor_copy(*deal_views(0))
+        x_codes = sb.tile([P, S], U32, name="x_codes", tag="w1_0", align_bytes=MX_ALIGN)
 
-        h_a = [sb.tile([P, HALF], F32, name="hA%d" % a) for a in range(2)]
-        for a in range(2):
-            acc = bank(a, "accA%d" % a, (P, HALF))
-            layer1(acc[:], wc_pair[0][:], ws_pair[0][:], slice(a * HALF, (a + 1) * HALF))
-            nc.scalar.activation(h_a[a][:], acc[:], GELU)
-        for a in range(2):
-            nc.vector.tensor_copy(up["A"][:].indirect(cell_sb[:, a * HC : (a + 1) * HC]), h_a[a][:])
+        def quantise_x(a):
+            cols = slice(a * PIECE, (a + 1) * PIECE)
+            quantise(x_codes[:, cols], x_scale[:, cols], x_bf[a][:].rearrange("p c j -> p (c j)"))
 
-        w_copy_cd(1)
-        quant(wc_cd[:], ws_cd[:], wg_cd[:].rearrange("p c j -> p (c j)"))
-        w_copy_pair(1)
-        quant(wc_pair[1][:], ws_pair[1][:], wg_pair[1][:].rearrange("p c j -> p (c j)"))
+        quantise_x(0)
+        quantise_w_pair(0)
+        quantise_x(1)
+        quantise_w_plane(0, 3)
+        quantise_w_plane(0, 2)
 
-        hs = {}
-        for n, b, wc, ws in (("C", 2, wc_cd[:, P : 2 * P], ws_cd[:, P : 2 * P]), ("B", 3, wc_pair[1][:], ws_pair[1][:]), ("D", 3, wc_cd[:, 0:P], ws_cd[:, 0:P])):
-            acc = bank(b, "acc" + n)
-            layer1(acc[:], wc, ws, slice(0, S))
-            hs[n] = sb.tile([P, S], F32, name="h" + n)
-            nc.scalar.activation(hs[n][:], acc[:], GELU)
+        def first_product(acc, n, cols):
+            nc.tensor.matmul_mx(
+                out=acc, lhsT=w1_codes[n][:].bitcast(FP8X4), lhsT_scale=w1_scale[n][:],
+                rhs=x_codes[:, cols].bitcast(FP8X4), rhs_scale=x_scale[:, cols], start=True, stop=True,
+            )
 
-        def turn_sum(n, banks):
-            sums = []
-            for half, b in enumerate(banks):
-                acc = bank(b, "sum%s%d" % (n, half), (P, 4, P))
-                for i in range(4):
-                    cells = slice(half * BANK + i * P, half * BANK + (i + 1) * P)
-                    nc.tensor.matmul(acc[:, i, :], skip_sb[n][:, cells], ident[:], start=(i == 0), stop=False, is_transpose=True)
-                sums.append(acc)
-            for half, acc in enumerate(sums):
-                for i in range(4):
-                    cells = slice(half * BANK + i * P, half * BANK + (i + 1) * P)
-                    nc.tensor.matmul(acc[:, i, :], up[n][:, cells], ident[:], start=False, stop=(i == 3), is_transpose=True)
-            return sums
+        def lo_piece(a, tag):
+            acc = bank(a, "acc_lo%d" % a, (P, PIECE))
+            first_product(acc[:], "lo", slice(a * PIECE, (a + 1) * PIECE))
+            act = sb.tile([P, PIECE], F32, name="h_lo%d" % a, tag=tag, align_bytes=MX_ALIGN)
+            nc.scalar.activation(act[:], acc[:], GELU, bias=no_bias[:])
+            nc.vector.tensor_copy(up["lo"][:].indirect(list_piece(cell_sb, a)), act[:])
 
-        zt = [sb.tile([P, 4, P], F32, name="zt%d" % b, tag="zt%d" % b, align_bytes=64) for b in range(2)]
-        stage = [sb.tile([P, 2, CH], F32, name="stage%d" % q) for q in range(NCH)]
+        lo_piece(0, "h_lo0")
+        nc.scalar.copy(*deal_views(1))
+        quantise_w_plane(1, 3)
+        quantise_w_pair(1)
+        quantise_w_plane(1, 2)
+        lo_piece(1, "w1_1")
 
-        def round_pair(h, sums):
-            for b in range(2):
-                dst = zt[b][:].bitcast(BF16).rearrange("c i (h m e) -> c h i m e", h=2, e=2)
-                nc.scalar.copy(dst[:, h], sums[b][:].rearrange("c i (e m) -> c i m e", e=2))
+        accs = {}
+        for n, b in (("plane3", 2), ("hi", 3), ("plane2", 4)):
+            accs[n] = bank(b, "acc_" + n)
+            first_product(accs[n][:], n, slice(0, S))
+        acts = {}
+        for n in ROW_TILES[1:]:
+            acts[n] = sb.tile([P, S], F32, name="h_" + n)
+            nc.scalar.activation(acts[n][:], accs[n][:], GELU, bias=no_bias[:])
 
-        def turn_back(src, banks, u):
-            for half, b in enumerate(banks):
-                acc = bank(b, "back%d%d" % (u, half))
-                for i in range(4):
-                    nc.tensor.transpose(acc[:, i * P : (i + 1) * P], src[half][:, i, :], ident[:])
-                for r in range(2):
-                    nc.scalar.copy(stage[2 * half + r][:, u, :], acc[:, r * CH : (r + 1) * CH])
+        def scatter(n):
+            nc.vector.tensor_copy(up[n][:].indirect(cell_sb[:]), acts[n][:])
 
-        sums_a = turn_sum("A", (2, 3))
-        round_pair(0, sums_a)
+        pairs_t = [sb.tile([P, TURNS, P], F32, name="pairs_t%d" % b, tag="pairs_t%d" % b, align_bytes=MX_ALIGN) for b in range(2)]
+        pairs = [sb.tile([P, 2, CHUNK], F32, name="pairs%d" % q) for q in range(CHUNKS)]
 
-        nc.vector.tensor_copy(up["C"][:].indirect(cell_sb[:]), hs["C"][:])
-        sums_c = turn_sum("C", (5, 6))
-        for b in range(2):
-            dst = ztc[b][:].bitcast(BF16).rearrange("c i (m e) -> c i m e", e=2)
-            nc.scalar.copy(dst[:, :, :, 1], sums_c[b][:])
-        turn_back(ztc, (0, 1), 1)
+        def add_skip_turned(h, banks):
+            n = ("lo", "hi")[h]
+            sums = [bank(b, "sum_%s%d" % (n, b), (P, TURNS, P)) for b in banks]
+            for source, first in ((skip_pair[n], True), (up[n], False)):
+                for b, acc in enumerate(sums):
+                    for i in range(TURNS):
+                        cells = slice(b * BANK + i * P, b * BANK + (i + 1) * P)
+                        nc.tensor.matmul(
+                            acc[:, i, :], source[:, cells], ident[:],
+                            start=first and i == 0, stop=not first and i == TURNS - 1, is_transpose=True,
+                        )
+            for b, acc in enumerate(sums):
+                halves = pairs_t[b][:].bitcast(BF16).rearrange("c i (h m e) -> c h i m e", h=2, e=2)
+                nc.scalar.copy(halves[:, h], acc[:].rearrange("c i (e m) -> c i m e", e=2))
 
-        nc.vector.tensor_copy(up["B"][:].indirect(cell_sb[:]), hs["B"][:])
-        sums_b = turn_sum("B", (5, 6))
-        round_pair(1, sums_b)
-        turn_back(zt, (2, 3), 0)
+        def turn_pairs_back(banks):
+            turned = [bank(b, "back%d" % b) for b in banks]
+            for b, acc in enumerate(turned):
+                for i in range(TURNS):
+                    nc.tensor.transpose(acc[:, i * P : (i + 1) * P], pairs_t[b][:, i, :], ident[:])
+            for q in range(CHUNKS):
+                b, r = divmod(q, BANK // CHUNK)
+                nc.scalar.copy(pairs[q][:, 0, :], turned[b][:, r * CHUNK : (r + 1) * CHUNK])
 
-        nc.vector.tensor_copy(up["D"][:].indirect(cell_sb[:]), hs["D"][:])
+        add_skip_turned(0, (3, 4))
+        scatter("plane3")
+        nc.scalar.copy(up["plane2"][:, U : 2 * U], up["plane3"][:])
+        scatter("hi")
+        add_skip_turned(1, (7, 6))
+        turn_pairs_back((3, 4))
+        scatter("plane2")
 
-        zg_all = sb.tile([P, 2 * U], F32, name="zg_all", tag="zt1", align_bytes=64)
-        zg = [zg_all[:, 2 * CH * q : 2 * CH * (q + 1)] for q in range(NCH)]
-        zc = [sb.tile([P, CH], U32, name="zc%d" % q, align_bytes=64) for q in range(NCH)]
-        zs = [sb.tile([P, CH], U8, name="zs%d" % q, align_bytes=64) for q in range(NCH)]
-        out_rows = out.rearrange("(a m) v -> m a v", a=2)
+        z_words = sb.tile([P, 2 * U], F32, name="z_words", tag="pairs_t1", align_bytes=MX_ALIGN)
+        z_codes = [sb.tile([P, CHUNK], U32, name="z_codes%d" % q, align_bytes=MX_ALIGN) for q in range(CHUNKS)]
+        z_scale = [sb.tile([P, CHUNK], U8, name="z_scale%d" % q, align_bytes=MX_ALIGN) for q in range(CHUNKS)]
 
-        def add_last(q):
-            cells = slice(q * CH, (q + 1) * CH)
-            dst = stage[q][:, 1, :].bitcast(BF16).rearrange("p (c e) -> p c e", e=2)
-            nc.vector.tensor_tensor(dst[:, :, 0], up["D"][:, cells], skip_sb["D"][:, cells], ADD)
+        def z_chunk(q):
+            return z_words[:, 2 * CHUNK * q : 2 * CHUNK * (q + 1)]
 
-        def weave(q):
-            nc.scalar.copy(zg[q].rearrange("p (c u) -> p c u", u=2), stage[q][:].rearrange("p u c -> p c u"))
+        def add_planes_23(q):
+            cells = slice(q * CHUNK, (q + 1) * CHUNK)
+            halves = pairs[q][:, 1, :].bitcast(BF16).rearrange("p (g i e) -> p g e i", i=LINE, e=2)
+            ups = up["plane2"][:].rearrange("p (e c) -> p e c", e=2)[:, :, cells].rearrange("p e (g i) -> p g e i", i=LINE)
+            nc.vector.tensor_tensor(halves, ups, skip_23[:, :, cells].rearrange("p e (g i) -> p g e i", i=LINE), ADD)
 
-        def quant_z(q):
-            quant(zc[q][:], zs[q][:], zg[q].bitcast(BF16))
-
-        def mm2(acc, a, q):
+        def second_product(acc, a, q):
             m = slice(a * P, (a + 1) * P)
-            nc.tensor.matmul_mx(out=acc, lhsT=w2c[:, m].bitcast(FP8X4), lhsT_scale=w2s[:, m], rhs=zc[q][:].bitcast(FP8X4), rhs_scale=zs[q][:], start=True, stop=True)
+            nc.tensor.matmul_mx(
+                out=acc, lhsT=w2_codes[:, m].bitcast(FP8X4), lhsT_scale=w2_scale[:, m],
+                rhs=z_codes[q][:].bitcast(FP8X4), rhs_scale=z_scale[q][:], start=True, stop=True,
+            )
 
-        def layer2(q, b, on_vector):
-            acc = bank(b, "o%d" % q, (P, 2, CH))
-            for a in range(2):
-                mm2(acc[:, a, :], a, q)
-            res = sb.tile([P, 2, CH], F32, name="res%d" % q)
-            if on_vector:
-                nc.vector.tensor_copy(res[:], acc[:])
-            else:
-                nc.scalar.copy(res[:], acc[:])
-            nc.sync.dma_start(out_rows[:, :, q * CH : (q + 1) * CH], res[:])
+        def finish(q, b, copy):
+            acc = bank(b, "out%d" % q, (P, N // P, CHUNK))
+            for a in range(N // P):
+                second_product(acc[:, a, :], a, q)
+            res = sb.tile([P, N // P, CHUNK], F32, name="res%d" % q)
+            copy(res[:], acc[:])
+            nc.sync.dma_start(out_rows[:, :, q * CHUNK : (q + 1) * CHUNK], res[:])
 
-        def layer2_split(q, banks):
-            for a in range(2):
-                acc = bank(banks[a], "o%d%d" % (q, a), (P, CH))
-                mm2(acc[:], a, q)
-                res = sb.tile([P, CH], F32, name="res%d%d" % (q, a))
-                if a == 0:
-                    nc.scalar.copy(res[:], acc[:])
-                else:
-                    nc.vector.tensor_copy(res[:], acc[:])
-                nc.sync.dma_start(out_rows[:, a, q * CH : (q + 1) * CH], res[:])
+        def finish_split(q, banks):
+            for a, copy in enumerate((nc.scalar.copy, nc.vector.tensor_copy)):
+                acc = bank(banks[a], "out%d_%d" % (q, a), (P, CHUNK))
+                second_product(acc[:], a, q)
+                res = sb.tile([P, CHUNK], F32, name="res%d_%d" % (q, a))
+                copy(res[:], acc[:])
+                nc.sync.dma_start(out_rows[:, a, q * CHUNK : (q + 1) * CHUNK], res[:])
 
-        for q in range(NCH):
-            add_last(q)
-            weave(q)
-        for q in range(NCH):
-            quant_z(q)
-        layer2(0, 7, False)
-        layer2(1, 4, True)
-        layer2(2, 0, False)
-        layer2_split(3, (1, 5))
+        for q in range(CHUNKS):
+            add_planes_23(q)
+            nc.scalar.copy(z_chunk(q).rearrange("p (c u) -> p c u", u=2), pairs[q][:].rearrange("p u c -> p c u"))
+        for q in range(CHUNKS):
+            quantise(z_codes[q][:], z_scale[q][:], z_chunk(q).bitcast(BF16))
+        finish(0, 5, nc.scalar.copy)
+        finish(1, 2, nc.vector.tensor_copy)
+        finish(2, 0, nc.scalar.copy)
+        finish_split(CHUNKS - 1, (1, 7))

from contextlib import ExitStack

import concourse.mybir as mybir
from concourse.masks import make_identity

K, T, S, H, N, U = 512, 2048, 512, 512, 256, 1024
FLOPS = 2 * K * H * S + 2 * H * N * U

F32 = mybir.dt.float32
BF16 = mybir.dt.bfloat16
I32 = mybir.dt.int32
U32 = mybir.dt.uint32
U16 = mybir.dt.uint16
U8 = mybir.dt.uint8
FP8X4 = mybir.dt.float8_e4m3fn_x4
GELU = mybir.ActivationFunctionType.Gelu_apprx_tanh
ADD = mybir.AluOpType.add

P = 128
PACK = 4
GROUP = 16
HALF_P = P // 2
PIECE = S // 2
BANK = 512
TURNS = BANK // P
CHUNK = 256
CHUNKS = U // CHUNK
LINE = 4
MX_ALIGN = 64
ROW_TILES = ("lo", "plane3", "hi", "plane2")


def tile_picked_unet_gelu_e_kernel(tc, xT, w1, w2_words, w2_scales, skip, offs, cell, out):
    nc = tc.nc
    with ExitStack() as ctx:
        sb = ctx.enter_context(tc.tile_pool(name="sb", bufs=1))
        ps = ctx.enter_context(tc.psum_pool(name="ps", bufs=1))

        def bank(b, name, shape=(P, BANK)):
            return ps.tile(list(shape), F32, name=name, tag="bank%d" % b)

        def quantise(codes, scales, values):
            nc.vector.quantize_mx(out=codes.bitcast(FP8X4), scales=scales, in_=values)

        def list_piece(lists, a):
            return lists[:, a * PIECE // GROUP : (a + 1) * PIECE // GROUP]

        offs_sb = sb.tile([P, S // GROUP], U16, name="offs_sb")
        cell_sb = sb.tile([P, S // GROUP], U16, name="cell_sb")
        x_sb = [sb.tile([P, T], F32, name="x%d" % j) for j in range(PACK)]
        w1_sb = [sb.tile([P, PACK, H // 2], F32, name="w1_%d" % h, tag="w1_%d" % h, align_bytes=MX_ALIGN) for h in range(2)]
        skip_pair = dict((n, sb.tile([P, U], F32, name="skip_" + n)) for n in ("lo", "hi"))
        skip_23 = sb.tile([P, 2, U], F32, name="skip_23")
        up = dict((n, sb.tile([P, 2 * U if n == "plane2" else U], F32, name="up_" + n)) for n in ROW_TILES)
        w2_codes = sb.tile([P, N], U32, name="w2_codes", align_bytes=MX_ALIGN)
        w2_scale = sb.tile([P, N], U8, name="w2_scale", align_bytes=MX_ALIGN)
        zero = sb.tile([P, 1], F32, name="zero")
        no_bias = sb.tile([P, 1], F32, name="no_bias")
        ident = sb.tile([P, P], F32, name="ident")

        x_rows = xT.rearrange("(p j) t -> p j t", j=PACK)
        w1_rows = w1.rearrange("(p j) c -> p j c", j=PACK)
        skip_rows = skip.rearrange("(p t) u -> p t u", t=PACK)
        out_rows = out.rearrange("(a m) v -> m a v", a=N // P)

        nc.vector.memset(zero[:], 0.0)
        nc.scalar.activation(no_bias[:], zero[:], GELU)
        nc.vector.memset(w2_scale[:].bitcast(I32), 0)
        for n in ROW_TILES:
            nc.vector.memset(up[n][:, 0:U], 0.0)
        make_identity(nc, ident[:])

        nc.sync.dma_start(x_sb[0][:], x_rows[:, 0, :])
        nc.sync.dma_start(offs_sb[:], offs)
        for j in range(1, PACK):
            nc.sync.dma_start(x_sb[j][:], x_rows[:, j, :])
        nc.sync.dma_start(w1_sb[0][:], w1_rows[:, :, 0 : H // 2])
        nc.sync.dma_start(cell_sb[:], cell)
        nc.sync.dma_start(w1_sb[1][:], w1_rows[:, :, H // 2 : H])
        for h, n in enumerate(("lo", "hi")):
            for e in range(2):
                nc.sync.dma_start(skip_pair[n][HALF_P * e : HALF_P * (e + 1), :], skip_rows[HALF_P * h : HALF_P * (h + 1), e, :])
        nc.sync.dma_start(skip_23[:], skip_rows[:, 2:4, :])
        nc.sync.dma_start(w2_codes[:].bitcast(I32), w2_words[0].rearrange("p n t -> p (n t)").bitcast(I32))
        for q in range(4):
            nc.sync.dma_start(w2_scale[32 * q : 32 * q + 4, :].bitcast(I32), w2_scales[0, 4 * q : 4 * q + 4, :].bitcast(I32))

        w_bf = [sb.tile([P, PACK, HALF_P, PACK], BF16, name="w_bf%d" % h, align_bytes=MX_ALIGN) for h in range(2)]
        w1_codes = dict((n, sb.tile([P, P], U32, name="w1_codes_" + n, align_bytes=MX_ALIGN)) for n in ROW_TILES)
        w1_scale = dict((n, sb.tile([P, P], U8, name="w1_scale_" + n, align_bytes=MX_ALIGN)) for n in ROW_TILES)

        def deal_views(h):
            return w_bf[h][:].rearrange("p t m j -> p m j t"), w1_sb[h][:].rearrange("p j (m t) -> p m j t", t=PACK)

        def quantise_w_pair(h):
            n = ("lo", "hi")[h]
            quantise(w1_codes[n][:], w1_scale[n][:], w_bf[h][:, 0:2].rearrange("p t m j -> p (t m j)"))

        def quantise_w_plane(h, t):
            n = "plane%d" % t
            cols = slice(HALF_P * h, HALF_P * (h + 1))
            quantise(w1_codes[n][:, cols], w1_scale[n][:, cols], w_bf[h][:, t].rearrange("p m j -> p (m j)"))

        x_bf = [sb.tile([P, PIECE, PACK], BF16, name="x_bf%d" % a, align_bytes=MX_ALIGN) for a in range(2)]
        x_scale = sb.tile([P, S], U8, name="x_scale", align_bytes=MX_ALIGN)
        for j in range(PACK):
            for a in range(2):
                picked = sb.tile([P, PIECE], BF16, name="picked%d%d" % (j, a))
                nc.vector.tensor_copy(picked[:], x_sb[j][:].indirect(list_piece(offs_sb, a)))
                nc.scalar.copy(x_bf[a][:, :, j], picked[:])

        nc.vector.tensor_copy(*deal_views(0))
        x_codes = sb.tile([P, S], U32, name="x_codes", tag="w1_0", align_bytes=MX_ALIGN)

        def quantise_x(a):
            cols = slice(a * PIECE, (a + 1) * PIECE)
            quantise(x_codes[:, cols], x_scale[:, cols], x_bf[a][:].rearrange("p c j -> p (c j)"))

        quantise_x(0)
        quantise_w_pair(0)
        quantise_x(1)
        quantise_w_plane(0, 3)
        quantise_w_plane(0, 2)

        def first_product(acc, n, cols):
            nc.tensor.matmul_mx(
                out=acc, lhsT=w1_codes[n][:].bitcast(FP8X4), lhsT_scale=w1_scale[n][:],
                rhs=x_codes[:, cols].bitcast(FP8X4), rhs_scale=x_scale[:, cols], start=True, stop=True,
            )

        def lo_piece(a, tag):
            acc = bank(a, "acc_lo%d" % a, (P, PIECE))
            first_product(acc[:], "lo", slice(a * PIECE, (a + 1) * PIECE))
            act = sb.tile([P, PIECE], F32, name="h_lo%d" % a, tag=tag, align_bytes=MX_ALIGN)
            nc.scalar.activation(act[:], acc[:], GELU, bias=no_bias[:])
            nc.vector.tensor_copy(up["lo"][:].indirect(list_piece(cell_sb, a)), act[:])

        lo_piece(0, "h_lo0")
        nc.scalar.copy(*deal_views(1))
        quantise_w_plane(1, 3)
        quantise_w_pair(1)
        quantise_w_plane(1, 2)
        lo_piece(1, "w1_1")

        accs = {}
        for n, b in (("plane3", 2), ("hi", 3), ("plane2", 4)):
            accs[n] = bank(b, "acc_" + n)
            first_product(accs[n][:], n, slice(0, S))
        acts = {}
        for n in ROW_TILES[1:]:
            acts[n] = sb.tile([P, S], F32, name="h_" + n)
            nc.scalar.activation(acts[n][:], accs[n][:], GELU, bias=no_bias[:])

        def scatter(n):
            nc.vector.tensor_copy(up[n][:].indirect(cell_sb[:]), acts[n][:])

        pairs_t = [sb.tile([P, TURNS, P], F32, name="pairs_t%d" % b, tag="pairs_t%d" % b, align_bytes=MX_ALIGN) for b in range(2)]
        pairs = [sb.tile([P, 2, CHUNK], F32, name="pairs%d" % q) for q in range(CHUNKS)]

        def add_skip_turned(h, banks):
            n = ("lo", "hi")[h]
            sums = [bank(b, "sum_%s%d" % (n, b), (P, TURNS, P)) for b in banks]
            for source, first in ((skip_pair[n], True), (up[n], False)):
                for b, acc in enumerate(sums):
                    for i in range(TURNS):
                        cells = slice(b * BANK + i * P, b * BANK + (i + 1) * P)
                        nc.tensor.matmul(
                            acc[:, i, :], source[:, cells], ident[:],
                            start=first and i == 0, stop=not first and i == TURNS - 1, is_transpose=True,
                        )
            for b, acc in enumerate(sums):
                halves = pairs_t[b][:].bitcast(BF16).rearrange("c i (h m e) -> c h i m e", h=2, e=2)
                nc.scalar.copy(halves[:, h], acc[:].rearrange("c i (e m) -> c i m e", e=2))

        def turn_pairs_back(banks):
            turned = [bank(b, "back%d" % b) for b in banks]
            for b, acc in enumerate(turned):
                for i in range(TURNS):
                    nc.tensor.transpose(acc[:, i * P : (i + 1) * P], pairs_t[b][:, i, :], ident[:])
            for q in range(CHUNKS):
                b, r = divmod(q, BANK // CHUNK)
                nc.scalar.copy(pairs[q][:, 0, :], turned[b][:, r * CHUNK : (r + 1) * CHUNK])

        add_skip_turned(0, (3, 4))
        scatter("plane3")
        nc.scalar.copy(up["plane2"][:, U : 2 * U], up["plane3"][:])
        scatter("hi")
        add_skip_turned(1, (7, 6))
        turn_pairs_back((3, 4))
        scatter("plane2")

        z_words = sb.tile([P, 2 * U], F32, name="z_words", tag="pairs_t1", align_bytes=MX_ALIGN)
        z_codes = [sb.tile([P, CHUNK], U32, name="z_codes%d" % q, align_bytes=MX_ALIGN) for q in range(CHUNKS)]
        z_scale = [sb.tile([P, CHUNK], U8, name="z_scale%d" % q, align_bytes=MX_ALIGN) for q in range(CHUNKS)]

        def z_chunk(q):
            return z_words[:, 2 * CHUNK * q : 2 * CHUNK * (q + 1)]

        def add_planes_23(q):
            cells = slice(q * CHUNK, (q + 1) * CHUNK)
            halves = pairs[q][:, 1, :].bitcast(BF16).rearrange("p (g i e) -> p g e i", i=LINE, e=2)
            ups = up["plane2"][:].rearrange("p (e c) -> p e c", e=2)[:, :, cells].rearrange("p e (g i) -> p g e i", i=LINE)
            nc.vector.tensor_tensor(halves, ups, skip_23[:, :, cells].rearrange("p e (g i) -> p g e i", i=LINE), ADD)

        def second_product(acc, a, q):
            m = slice(a * P, (a + 1) * P)
            nc.tensor.matmul_mx(
                out=acc, lhsT=w2_codes[:, m].bitcast(FP8X4), lhsT_scale=w2_scale[:, m],
                rhs=z_codes[q][:].bitcast(FP8X4), rhs_scale=z_scale[q][:], start=True, stop=True,
            )

        def finish(q, b, copy):
            acc = bank(b, "out%d" % q, (P, N // P, CHUNK))
            for a in range(N // P):
                second_product(acc[:, a, :], a, q)
            res = sb.tile([P, N // P, CHUNK], F32, name="res%d" % q)
            copy(res[:], acc[:])
            nc.sync.dma_start(out_rows[:, :, q * CHUNK : (q + 1) * CHUNK], res[:])

        def finish_split(q, banks):
            for a, copy in enumerate((nc.scalar.copy, nc.vector.tensor_copy)):
                acc = bank(banks[a], "out%d_%d" % (q, a), (P, CHUNK))
                second_product(acc[:], a, q)
                res = sb.tile([P, CHUNK], F32, name="res%d_%d" % (q, a))
                copy(res[:], acc[:])
                nc.sync.dma_start(out_rows[:, a, q * CHUNK : (q + 1) * CHUNK], res[:])

        for q in range(CHUNKS):
            add_planes_23(q)
            nc.scalar.copy(z_chunk(q).rearrange("p (c u) -> p c u", u=2), pairs[q][:].rearrange("p u c -> p c u"))
        for q in range(CHUNKS):
            quantise(z_codes[q][:], z_scale[q][:], z_chunk(q).bitcast(BF16))
        finish(0, 5, nc.scalar.copy)
        finish(1, 2, nc.vector.tensor_copy)
        finish(2, 0, nc.scalar.copy)
        finish_split(CHUNKS - 1, (1, 7))
